import numpy as np
import ml_dtypes


def mxq(x, axis, fmt="e4m3"):
    dtype, down = {"e4m3": (ml_dtypes.float8_e4m3fn, 7), "e5m2": (ml_dtypes.float8_e5m2, 14)}[fmt]
    v = np.moveaxis(np.asarray(x, np.float32).astype(ml_dtypes.bfloat16).astype(np.float64), axis, -1)
    blocks = v.reshape(v.shape[:-1] + (-1, 32))
    amax = np.abs(blocks).max(-1, keepdims=True)
    byte = np.maximum(np.where(amax > 0, np.frexp(amax)[1] - 1 + 127, 0) - down, 1)
    scale = np.exp2(byte - 127.0)
    codes = (blocks / scale).astype(np.float32).astype(dtype).astype(np.float64)
    return np.moveaxis((codes * scale).reshape(v.shape), -1, axis)


WIDE = False


def mx_kscale(k):
    if not WIDE:
        return np.ones(k)
    levels = np.array([10, -10, 5, -5, 0])
    if k % 512:
        return np.exp2(np.random.permutation(np.resize(levels, k // 32))).repeat(32)
    a = np.empty((k // 512, 16))
    for p in range(k // 512):
        a[p, :8] = np.random.permutation(np.resize(levels, 8))
        for g in range(8):
            far = levels[np.abs(levels - a[p, g]) >= 10]
            a[p, g + 8] = far[np.random.randint(len(far))]
    return np.exp2(a.ravel()).repeat(32)


def f64(x):
    return np.asarray(x).astype(np.float64)


def striped(idx):
    return np.tile(idx.reshape(-1, 16).T, (8, 1)).astype(np.uint16)


def unstriped(offs):
    return offs[:16].T.reshape(-1).astype(np.int64)


E2M1 = np.array([0.0, 0.5, 1.0, 1.5, 2.0, 3.0, 4.0, 6.0, -0.0, -0.5, -1.0, -1.5, -2.0, -3.0, -4.0, -6.0])


def pack_weight(w, fmt):
    k, n = w.shape
    w = f64(np.asarray(w, np.float32).astype(ml_dtypes.bfloat16)).reshape(k // 32, 32, n)
    amax = np.abs(w).max(1)
    if fmt == "e4m3":
        byte = np.frexp(amax)[1] - 1 + 127 - 7
    else:
        mant, ex = np.frexp(amax / 6.0)
        byte = np.where(mant > 0.5, ex, ex - 1) + 127
    byte = np.clip(np.where(amax > 0, byte, 1), 1, 254)
    scaled = (w * np.exp2(127.0 - byte)[:, None, :]).reshape(k, n).astype(np.float32)
    by_word = np.ascontiguousarray(scaled.reshape(k // 512, 128, 4, n).transpose(0, 1, 3, 2))
    if fmt == "e4m3":
        words = by_word.astype(ml_dtypes.float8_e4m3fn).view(np.uint8)
    else:
        c = by_word.astype(ml_dtypes.float4_e2m1fn).view(np.uint8) & 0xF
        words = (c[..., 0::2] | (c[..., 1::2] << 4)).reshape(k // 512, 128, 2 * n)
    return np.ascontiguousarray(words), np.ascontiguousarray(byte.astype(np.uint8).reshape(k // 512, 16, n))


def unpack_weight(words, scales, fmt):
    g, _, n = scales.shape
    words = np.ascontiguousarray(words).reshape(g, 128, n, -1)
    if fmt == "e4m3":
        vals = words.view(ml_dtypes.float8_e4m3fn).astype(np.float64)
    else:
        nib = np.empty((g, 128, n, 4), np.uint8)
        nib[..., 0::2] = words & 0xF
        nib[..., 1::2] = words >> 4
        vals = E2M1[nib]
    vals = vals * np.repeat(np.exp2(scales.astype(np.float64) - 127.0), 8, axis=1)[..., None]
    return vals.transpose(0, 1, 3, 2).reshape(g * 512, n)


def gelu(v):
    return 0.5 * v * (1.0 + np.tanh(np.sqrt(2.0 / np.pi) * (v + 0.044715 * v**3)))


def striped8(idx):
    return np.concatenate([v.reshape(-1, 16).T for v in idx]).astype(np.uint16)


def unstriped8(offs):
    return np.stack([offs[16 * g:16 * g + 16].T.reshape(-1) for g in range(8)]).astype(np.int64)


def runs(v, idx8):
    k = np.arange(v.shape[0])
    return v[k[:, None], idx8[k % 512 // 64]]


def often(T, S):
    return np.random.permutation(T)[(T * np.random.uniform(0, 1, S) ** 4).astype(np.int64)]


K, H, N, T, S, P = 1024, 1024, 512, 2048, 1024, 512

def setup_inputs():
    n = np.random.standard_normal
    s = mx_kscale(K)[:, None]
    u = mx_kscale(H)[:, None]
    d = {}
    d["tab_words"], d["tab_scales"] = pack_weight(n((K, T)) * s, "e4m3")
    d["offs"] = striped8(np.stack([often(T, S) for _ in range(8)]))
    d["pos1"] = striped(np.random.permutation(S)[:P])
    d["pos2"] = striped(np.random.permutation(S)[:P])
    d["w1"] = (n((K, H)) / K**0.5 / s * u.T).astype(np.float32)
    d["w2_words"], d["w2_scales"] = pack_weight(1.8 * n((K, H)) / K**0.5 / s, "e2m1")
    d["gain"] = (np.exp(0.3 * n(H)) * u[:, 0]).astype(np.float32)
    d["base"] = ((1.2 + 0.8 * n((H, P))) * u).astype(np.float32)
    d["w3"] = (0.8 * n((H, N)) / H**0.5 / u).astype(np.float32)
    return d

def reference(tab_words, tab_scales, offs, pos1, pos2, w1, w2_words, w2_scales, gain, base, w3):
    v = runs(unpack_weight(tab_words, tab_scales, "e4m3"), unstriped8(offs))
    a = mxq(f64(w1), 0, "e4m3").T @ v
    b = unpack_weight(w2_words, w2_scales, "e2m1").T @ v
    silu_b = b / (1.0 + np.exp(-b))
    h = a + f64(gain)[:, None] * silu_b
    z = np.maximum(h[:, unstriped(pos1)], h[:, unstriped(pos2)]) - f64(base)
    y = mxq(f64(w3), 0, "e4m3").T @ mxq(z, 0, "e4m3")
    return np.square(y)

@@ -1,0 +1,337 @@
+from contextlib import ExitStack
+
+import concourse.mybir as mybir
+from concourse.masks import make_identity
+
+K, H, N, T, S, PAIRS = 1024, 1024, 512, 2048, 1024, 512
+FLOPS = 2 * K * H * S * 2 + 2 * H * N * PAIRS
+
+F32 = mybir.dt.float32
+BF16 = mybir.dt.bfloat16
+I32 = mybir.dt.int32
+U32 = mybir.dt.uint32
+U16 = mybir.dt.uint16
+U8 = mybir.dt.uint8
+FP8X4 = mybir.dt.float8_e4m3fn_x4
+FP4X4 = mybir.dt.float4_e2m1fn_x4
+ALU = mybir.AluOpType
+ACT = mybir.ActivationFunctionType
+
+P = 128
+BANK = 512
+HALF = PAIRS // 2
+FIRST_ROW = 12
+
+
+def tile_list_cue_crowding_scores_kernel(
+    tc, tab_words, tab_scales, offs, pos1, pos2, w1, w2_words, w2_scales, gain, base, w3, out
+):
+    nc = tc.nc
+    with ExitStack() as ctx:
+        keep = ctx.enter_context(tc.tile_pool(name="keep", bufs=1))
+        ring = ctx.enter_context(tc.tile_pool(name="ring", bufs=2))
+        psum = ctx.enter_context(tc.psum_pool(name="psum", bufs=1))
+
+        def held(name, shape, dtype):
+            return keep.tile(shape, dtype, name=name, align_bytes=64)
+
+        def bank(n, width=BANK):
+            return psum.tile([P, width], F32, name="bank%d" % n, tag="bank%d" % n)
+
+        def slot_rows(x, b, t):
+            return x[512 * b : 512 * (b + 1), :].rearrange("(g t q) m -> g t q m", t=4, q=8)[:, t, :, :]
+
+        offs_sb = held("offs_sb", [P, S // 16], U16)
+        pos1_sb = held("pos1_sb", [P, PAIRS // 16], U16)
+        pos2_sb = held("pos2_sb", [P, PAIRS // 16], U16)
+        nc.sync.dma_start(offs_sb[:], offs)
+
+        tab_rows = held("tab_rows", [P, T], U8)
+        nc.vector.memset(tab_rows[:].bitcast(I32), 0)
+        for d in range(4):
+            nc.scalar.dma_start(
+                tab_rows[32 * d + FIRST_ROW : 32 * d + FIRST_ROW + 8, :].bitcast(I32),
+                tab_scales[:, 4 * d : 4 * d + 4, :].rearrange("a r t -> r a t").bitcast(I32),
+            )
+        v_planes = held("v_planes", [P, 2 * S], U8)
+        nc.vector.memset(v_planes[:].bitcast(I32), 0)
+
+        tab_sb = []
+        for a in range(2):
+            words = held("tab_sb%d" % a, [P, T], I32)
+            nc.sync.dma_start(words[:], tab_words[a].rearrange("p t i -> p (t i)").bitcast(I32))
+            tab_sb.append(words)
+
+        w2_raw = held("w2_raw", [P, H], I32)
+        nc.sync.dma_start(w2_raw[:].rearrange("p (a c) -> p a c", a=2), w2_words.rearrange("a p c -> p a c").bitcast(I32))
+        w2_rows = held("w2_rows", [P, 2 * H], U8)
+        nc.gpsimd.memset(w2_rows[:].bitcast(I32), 0)
+        for d in range(4):
+            nc.gpsimd.dma_start(
+                w2_rows[32 * d : 32 * d + 4, :].bitcast(I32).rearrange("r (a c) -> r a c", a=2),
+                w2_scales[:, 4 * d : 4 * d + 4, :].rearrange("a r c -> r a c").bitcast(I32),
+            )
+
+        gain_rows = held("gain_rows", [P, P], F32)
+        nc.vector.memset(gain_rows[:], 0.0)
+        ident = held("ident", [P, P], F32)
+        make_identity(nc, ident[:])
+
+        w1_raw = {}
+        base_sb = {}
+        w3_raw = {}
+
+        def load_w1(b):
+            for a in range(2):
+                w1_raw[b, a] = held("w1_raw%d%d" % (b, a), [P, 4, 512], F32)
+                rows = w1[512 * a : 512 * (a + 1), 512 * b : 512 * (b + 1)]
+                nc.sync.dma_start(w1_raw[b, a][:], rows.rearrange("(p j) c -> p j c", j=4))
+
+        def load_base(b):
+            for t in range(4):
+                base_sb[4 * b + t] = held("base_sb%d" % (4 * b + t), [P, PAIRS], F32)
+                nc.sync.dma_start(base_sb[4 * b + t][:], slot_rows(base, b, t))
+
+        def load_w3(b):
+            w3_raw[b] = held("w3_raw%d" % b, [P, 4, N], F32)
+            for t in range(4):
+                nc.sync.dma_start(w3_raw[b][:, t, :], slot_rows(w3, b, t))
+
+        load_w1(0)
+        nc.sync.dma_start(pos1_sb[:], pos1)
+        nc.sync.dma_start(pos2_sb[:], pos2)
+        load_base(0)
+        load_w1(1)
+        load_base(1)
+        load_w3(0)
+        load_w3(1)
+
+        picked_rows = held("picked_rows", [P, S], U8)
+        nc.vector.tensor_copy(picked_rows[:], tab_rows[:].indirect(offs_sb[:]))
+        for d in range(4):
+            nc.scalar.dma_start(
+                v_planes[32 * d : 32 * d + 4, :].bitcast(I32).rearrange("r (a s) -> r a s", a=2),
+                picked_rows[32 * d + FIRST_ROW : 32 * d + FIRST_ROW + 8, :].bitcast(I32),
+            )
+        for b in range(2):
+            nc.scalar.dma_start(
+                gain_rows[4 * b : 4 * b + 4, :].rearrange("t (g q) -> t g q", q=8),
+                gain[512 * b : 512 * (b + 1)].rearrange("(g t q) -> t g q", t=4, q=8),
+            )
+        v_words = []
+        for a in range(2):
+            picked = held("v_words%d" % a, [P, S], U32)
+            nc.vector.tensor_copy(picked[:], tab_sb[a][:].bitcast(U32).indirect(offs_sb[:]))
+            v_words.append(picked)
+
+        w2_codes = held("w2_codes", [P, 4 * H], U8)
+        nc.vector.tensor_copy(
+            w2_codes[:].bitcast(I32).rearrange("p (c t g w) -> p c t g w", t=4, g=16, w=4),
+            w2_raw[:].rearrange("p (c g t w) -> p c t g w", t=4, g=16, w=4),
+        )
+        w2_planes = held("w2_planes", [P, 2 * H], U8)
+        nc.vector.tensor_copy(
+            w2_planes[:].bitcast(I32).rearrange("p (c t g w) -> p c t g w", t=4, g=16, w=2),
+            w2_rows[:].bitcast(I32).rearrange("p (c g t w) -> p c t g w", t=4, g=16, w=2),
+        )
+
+        gain_sb = held("gain_sb", [P, 8], F32)
+
+        def copy_on(engine, dst, src):
+            if engine == "vector":
+                nc.vector.tensor_copy(dst, src)
+            else:
+                nc.scalar.copy(dst, src)
+
+        def quantize(name, rounded, width):
+            codes = held(name + "_codes", [P, width], U32)
+            plane = held(name + "_plane", [P, width], U8)
+            nc.vector.quantize_mx(out=codes[:].bitcast(FP8X4), scales=plane[:], in_=rounded)
+            return codes, plane
+
+        w1_round = {}
+        w1_mx = {}
+
+        def round_w1(b, a, slots, engine):
+            rounded = held("w1_round%d%d%d" % (b, a, slots[0]), [P, 512 * len(slots)], BF16)
+            src = w1_raw[b, a][:].rearrange("p j (g t u i) -> p t g u j i", t=4, u=2, i=4)
+            for n, t in enumerate(slots):
+                dst = rounded[:, 512 * n : 512 * (n + 1)].rearrange("p (g u i j) -> p g u j i", u=2, i=4, j=4)
+                copy_on(engine, dst, src[:, t])
+            w1_round[b, a, slots[0]] = rounded
+
+        def quantize_w1(b, a, slots):
+            codes, plane = quantize("w1_%d%d%d" % (b, a, slots[0]), w1_round[b, a, slots[0]][:], P * len(slots))
+            for n, t in enumerate(slots):
+                w1_mx[4 * b + t, a] = (codes[:, P * n : P * (n + 1)], plane[:, P * n : P * (n + 1)])
+
+        def product(acc, lhs, lhs_plane, a, c):
+            nc.tensor.matmul_mx(
+                out=acc[:],
+                lhsT=lhs,
+                lhsT_scale=lhs_plane,
+                rhs=v_words[a][:, BANK * c : BANK * (c + 1)].bitcast(FP8X4),
+                rhs_scale=v_planes[:, S * a + BANK * c : S * a + BANK * (c + 1)],
+                start=(a == 0),
+                stop=(a == 1),
+            )
+
+        silu_sb = {}
+        lin = {}
+        h_sb = {}
+        picks = {}
+
+        def curved(i):
+            silu_sb[i] = ring.tile([P, S], F32, name="silu_sb", bufs=4)
+            for c in range(2):
+                acc = bank(4 + 2 * (i % 2) + c)
+                for a in range(2):
+                    col = H * a + P * i
+                    product(acc, w2_codes[:, 2 * col : 2 * (col + P)].bitcast(FP4X4), w2_planes[:, col : col + P], a, c)
+                nc.scalar.activation(silu_sb[i][:, BANK * c : BANK * (c + 1)], acc[:], ACT.Silu)
+
+        def linear(i):
+            for c in range(2):
+                lin[i, c] = bank(2 * (i % 2) + c)
+                for a in range(2):
+                    codes, plane = w1_mx[i, a]
+                    product(lin[i, c], codes.bitcast(FP8X4), plane, a, c)
+
+        def features(i):
+            h_sb[i] = ring.tile([P, S], F32, name="h_sb", bufs=3, align_bytes=64)
+            for c in range(2):
+                cols = slice(BANK * c, BANK * (c + 1))
+                nc.vector.scalar_tensor_tensor(
+                    h_sb[i][:, cols], silu_sb[i][:, cols], gain_sb[:, i : i + 1], lin[i, c][:], ALU.mult, ALU.add
+                )
+
+        def pick(i, lo, hi):
+            both = []
+            for name, pos in (("pick1", pos1_sb), ("pick2", pos2_sb)):
+                got = ring.tile([P, hi - lo], F32, name=name, align_bytes=64)
+                nc.vector.tensor_tensor(
+                    got[:], h_sb[i][:].indirect(pos[:, lo // 16 : hi // 16]), base_sb[i][:, lo:hi], ALU.subtract
+                )
+                both.append(got)
+            picks[i, lo] = both
+
+        z_rows = [held("z_rows%d" % b, [P, 2, 4, HALF], BF16) for b in range(2)]
+
+        def larger(i, lo, hi):
+            one, two = picks[i, lo]
+            halves = slice(lo // HALF, hi // HALF)
+            nc.vector.tensor_tensor(
+                z_rows[i // 4][:, halves, i % 4, :],
+                one[:].rearrange("p (h c) -> p h c", c=HALF),
+                two[:].rearrange("p (h c) -> p h c", c=HALF),
+                ALU.max,
+            )
+
+        z_round = {}
+        z_mx = {}
+
+        def weave_z(b, halves, engine):
+            woven = held("z_round%d%d" % (b, halves[0]), [P, 4 * HALF * len(halves)], BF16)
+            copy_on(
+                engine,
+                woven[:].rearrange("p (h c i t) -> p h c t i", c=HALF // 4, i=4, t=4),
+                z_rows[b][:, halves[0] : halves[-1] + 1].rearrange("p h t (c i) -> p h c t i", i=4),
+            )
+            z_round[b, halves[0]] = woven
+
+        def quantize_z(b, halves):
+            codes, plane = quantize("z_%d%d" % (b, halves[0]), z_round[b, halves[0]][:], HALF * len(halves))
+            for n, half in enumerate(halves):
+                z_mx[b, half] = (codes[:, HALF * n : HALF * (n + 1)], plane[:, HALF * n : HALF * (n + 1)])
+
+        w3_round = {}
+        w3_mx = {}
+
+        def round_w3(b):
+            w3_round[b] = held("w3_round%d" % b, [P, 4 * N], BF16)
+            for c in range(2):
+                nc.scalar.copy(
+                    w3_round[b][:, 2 * N * c : 2 * N * (c + 1)].rearrange("p (c i t) -> p c t i", i=4, t=4),
+                    w3_raw[b][:, :, N // 2 * c : N // 2 * (c + 1)].rearrange("p t (c i) -> p c t i", i=4),
+                )
+
+        def quantize_w3(b):
+            w3_mx[b] = quantize("w3_%d" % b, w3_round[b][:], N)
+
+        score = {}
+
+        def second(b, half):
+            z_codes, z_plane = z_mx[b, half]
+            codes, plane = w3_mx[b]
+            for n in range(4):
+                if b == 0:
+                    score[n, half] = bank((4 + 4 * half + n) % 8, HALF)
+                nc.tensor.matmul_mx(
+                    out=score[n, half][:],
+                    lhsT=codes[:, P * n : P * (n + 1)].bitcast(FP8X4),
+                    lhsT_scale=plane[:, P * n : P * (n + 1)],
+                    rhs=z_codes.bitcast(FP8X4),
+                    rhs_scale=z_plane,
+                    start=(b == 0),
+                    stop=(b == 1),
+                )
+
+        def finish(half):
+            out_rows = out.rearrange("(n p) m -> p n m", p=P)
+            for pair in range(2):
+                squared = held("squared%d%d" % (half, pair), [P, 2, HALF], F32)
+                for n in range(2):
+                    nc.scalar.activation(squared[:, n, :], score[2 * pair + n, half][:], ACT.Square)
+                nc.sync.dma_start(out_rows[:, 2 * pair : 2 * pair + 2, HALF * half : HALF * (half + 1)], squared[:])
+
+        every = (0, 1, 2, 3)
+        round_w1(0, 0, every, "vector")
+        curved(0)
+        gain_bank = bank(0, P)
+        nc.tensor.transpose(gain_bank[:], gain_rows[:], ident[:])
+        nc.scalar.copy(gain_sb[:], gain_bank[:, 0:8])
+        quantize_w1(0, 0, every)
+        round_w1(0, 1, (0,), "vector")
+        round_w1(0, 1, (1,), "scalar")
+        quantize_w1(0, 1, (0,))
+        linear(0)
+        curved(1)
+        quantize_w1(0, 1, (1,))
+        linear(1)
+        round_w1(0, 1, (2, 3), "scalar")
+        features(0)
+        curved(2)
+        quantize_w1(0, 1, (2, 3))
+        for i in range(7):
+            pick(i, 0, PAIRS)
+            features(i + 1)
+            if i + 2 < 8:
+                linear(i + 2)
+            if i + 3 < 8:
+                curved(i + 3)
+            larger(i, 0, PAIRS)
+            if i < 2:
+                round_w1(1, i, every, "scalar")
+                quantize_w1(1, i, every)
+            if i == 3:
+                weave_z(0, (0, 1), "scalar")
+            if i in (3, 4):
+                round_w3(i - 3)
+            if i == 4:
+                quantize_z(0, (0, 1))
+            if i in (4, 5):
+                quantize_w3(i - 4)
+        second(0, 0)
+        second(0, 1)
+        pick(7, 0, HALF)
+        larger(7, 0, HALF)
+        weave_z(1, (0,), "scalar")
+        pick(7, HALF, PAIRS)
+        larger(7, HALF, PAIRS)
+        quantize_z(1, (0,))
+        weave_z(1, (1,), "vector")
+        second(1, 0)
+        finish(0)
+        quantize_z(1, (1,))
+        second(1, 1)
+        finish(1)

@@ -20,7 +20,6 @@ ACT = mybir.ActivationFunctionType
 P = 128
 BANK = 512
 HALF = PAIRS // 2
-FIRST_ROW = 12
 
 
 def tile_list_cue_crowding_scores_kernel(
@@ -32,8 +31,8 @@ def tile_list_cue_crowding_scores_kernel(
         ring = ctx.enter_context(tc.tile_pool(name="ring", bufs=2))
         psum = ctx.enter_context(tc.psum_pool(name="psum", bufs=1))
 
-        def held(name, shape, dtype):
-            return keep.tile(shape, dtype, name=name, align_bytes=64)
+        def held(name, shape, dtype, slot=None):
+            return keep.tile(shape, dtype, name=name, tag=slot or name, align_bytes=64)
 
         def bank(n, width=BANK):
             return psum.tile([P, width], F32, name="bank%d" % n, tag="bank%d" % n)
@@ -45,78 +44,70 @@ def tile_list_cue_crowding_scores_kernel(
         pos1_sb = held("pos1_sb", [P, PAIRS // 16], U16)
         pos2_sb = held("pos2_sb", [P, PAIRS // 16], U16)
         nc.sync.dma_start(offs_sb[:], offs)
+        nc.sync.dma_start(pos1_sb[:], pos1)
+        nc.sync.dma_start(pos2_sb[:], pos2)
 
         tab_rows = held("tab_rows", [P, T], U8)
-        nc.vector.memset(tab_rows[:].bitcast(I32), 0)
+        w2_rows = held("w2_rows", [P, 2 * H], U8)
+        gain_rows = held("gain_rows", [P, P], F32)
+        v_planes = held("v_planes", [P, 2 * S], U8)
+        nc.gpsimd.memset(tab_rows[:].bitcast(I32), 0)
+        nc.gpsimd.memset(w2_rows[:].bitcast(I32), 0)
+        nc.gpsimd.memset(gain_rows[:], 0.0)
+        nc.gpsimd.memset(v_planes[:].bitcast(I32), 0)
+        ident = held("ident", [P, P], F32)
+        make_identity(nc, ident[:])
+        nc.scalar.dma_start(tab_rows[0:P:4, :].bitcast(I32), tab_scales.rearrange("a q t -> q a t").bitcast(I32))
         for d in range(4):
             nc.scalar.dma_start(
-                tab_rows[32 * d + FIRST_ROW : 32 * d + FIRST_ROW + 8, :].bitcast(I32),
-                tab_scales[:, 4 * d : 4 * d + 4, :].rearrange("a r t -> r a t").bitcast(I32),
-            )
-        v_planes = held("v_planes", [P, 2 * S], U8)
-        nc.vector.memset(v_planes[:].bitcast(I32), 0)
-
-        tab_sb = []
-        for a in range(2):
-            words = held("tab_sb%d" % a, [P, T], I32)
-            nc.sync.dma_start(words[:], tab_words[a].rearrange("p t i -> p (t i)").bitcast(I32))
-            tab_sb.append(words)
-
-        w2_raw = held("w2_raw", [P, H], I32)
-        nc.sync.dma_start(w2_raw[:].rearrange("p (a c) -> p a c", a=2), w2_words.rearrange("a p c -> p a c").bitcast(I32))
-        w2_rows = held("w2_rows", [P, 2 * H], U8)
-        nc.gpsimd.memset(w2_rows[:].bitcast(I32), 0)
-        for d in range(4):
-            nc.gpsimd.dma_start(
                 w2_rows[32 * d : 32 * d + 4, :].bitcast(I32).rearrange("r (a c) -> r a c", a=2),
                 w2_scales[:, 4 * d : 4 * d + 4, :].rearrange("a r c -> r a c").bitcast(I32),
             )
+        for b in range(2):
+            nc.scalar.dma_start(
+                gain_rows[4 * b : 4 * b + 4, :].rearrange("t (g q) -> t g q", q=8),
+                gain[512 * b : 512 * (b + 1)].rearrange("(g t q) -> t g q", t=4, q=8),
+            )
 
-        gain_rows = held("gain_rows", [P, P], F32)
-        nc.vector.memset(gain_rows[:], 0.0)
-        ident = held("ident", [P, P], F32)
-        make_identity(nc, ident[:])
+        tab_sb = {}
+
+        def load_table(a):
+            tab_sb[a] = held("tab_sb%d" % a, [P, T], I32)
+            nc.sync.dma_start(tab_sb[a][:], tab_words[a].rearrange("p t i -> p (t i)").bitcast(I32))
 
         w1_raw = {}
         base_sb = {}
         w3_raw = {}
 
-        def load_w1(b):
-            for a in range(2):
-                w1_raw[b, a] = held("w1_raw%d%d" % (b, a), [P, 4, 512], F32)
-                rows = w1[512 * a : 512 * (a + 1), 512 * b : 512 * (b + 1)]
-                nc.sync.dma_start(w1_raw[b, a][:], rows.rearrange("(p j) c -> p j c", j=4))
+        def load_w1(b, a, slot=None):
+            w1_raw[b, a] = held("w1_raw%d%d" % (b, a), [P, 4, 512], F32, slot)
+            rows = w1[512 * a : 512 * (a + 1), 512 * b : 512 * (b + 1)]
+            nc.sync.dma_start(w1_raw[b, a][:], rows.rearrange("(p j) c -> p j c", j=4))
 
-        def load_base(b):
+        def load_base(b, slot):
+            rows = held("base_sb%d" % b, [P, 4, PAIRS], F32, slot)
             for t in range(4):
-                base_sb[4 * b + t] = held("base_sb%d" % (4 * b + t), [P, PAIRS], F32)
-                nc.sync.dma_start(base_sb[4 * b + t][:], slot_rows(base, b, t))
+                base_sb[4 * b + t] = rows[:, t, :]
+                nc.sync.dma_start(rows[:, t, :], slot_rows(base, b, t))
 
-        def load_w3(b):
-            w3_raw[b] = held("w3_raw%d" % b, [P, 4, N], F32)
+        def load_w3(b, slot):
+            w3_raw[b] = held("w3_raw%d" % b, [P, 4, N], F32, slot)
             for t in range(4):
                 nc.sync.dma_start(w3_raw[b][:, t, :], slot_rows(w3, b, t))
 
-        load_w1(0)
-        nc.sync.dma_start(pos1_sb[:], pos1)
-        nc.sync.dma_start(pos2_sb[:], pos2)
-        load_base(0)
-        load_w1(1)
-        load_base(1)
-        load_w3(0)
-        load_w3(1)
+        load_table(0)
+        load_w1(0, 0)
+        load_table(1)
+        w2_raw = held("w2_raw", [P, H], I32)
+        nc.sync.dma_start(w2_raw[:].rearrange("p (a c) -> p a c", a=2), w2_words.rearrange("a p c -> p a c").bitcast(I32))
+        load_w1(0, 1)
 
         picked_rows = held("picked_rows", [P, S], U8)
         nc.vector.tensor_copy(picked_rows[:], tab_rows[:].indirect(offs_sb[:]))
         for d in range(4):
             nc.scalar.dma_start(
                 v_planes[32 * d : 32 * d + 4, :].bitcast(I32).rearrange("r (a s) -> r a s", a=2),
-                picked_rows[32 * d + FIRST_ROW : 32 * d + FIRST_ROW + 8, :].bitcast(I32),
-            )
-        for b in range(2):
-            nc.scalar.dma_start(
-                gain_rows[4 * b : 4 * b + 4, :].rearrange("t (g q) -> t g q", q=8),
-                gain[512 * b : 512 * (b + 1)].rearrange("(g t q) -> t g q", t=4, q=8),
+                picked_rows[32 * d : 32 * (d + 1) : 4, :].bitcast(I32),
             )
         v_words = []
         for a in range(2):
@@ -135,6 +126,7 @@ def tile_list_cue_crowding_scores_kernel(
             w2_rows[:].bitcast(I32).rearrange("p (c g t w) -> p c t g w", t=4, g=16, w=2),
         )
 
+        load_base(0, "picked_rows")
         gain_sb = held("gain_sb", [P, 8], F32)
 
         def copy_on(engine, dst, src):
@@ -176,13 +168,14 @@ def tile_list_cue_crowding_scores_kernel(
                 stop=(a == 1),
             )
 
-        silu_sb = {}
+        curve = held("curve", [P, 9 * S], F32)
+        silu_sb = [curve[:, S * i : S * (i + 1)] for i in range(8)]
+        z_rows = curve[:, S:].bitcast(BF16).rearrange("p (i m) -> p i m", i=8)
         lin = {}
         h_sb = {}
         picks = {}
 
         def curved(i):
-            silu_sb[i] = ring.tile([P, S], F32, name="silu_sb", bufs=4)
             for c in range(2):
                 acc = bank(4 + 2 * (i % 2) + c)
                 for a in range(2):
@@ -208,41 +201,31 @@ def tile_list_cue_crowding_scores_kernel(
         def pick(i, lo, hi):
             both = []
             for name, pos in (("pick1", pos1_sb), ("pick2", pos2_sb)):
-                got = ring.tile([P, hi - lo], F32, name=name, align_bytes=64)
+                got = ring.tile([P, hi - lo], F32, name=name, bufs=3, align_bytes=64)
                 nc.vector.tensor_tensor(
                     got[:], h_sb[i][:].indirect(pos[:, lo // 16 : hi // 16]), base_sb[i][:, lo:hi], ALU.subtract
                 )
                 both.append(got)
             picks[i, lo] = both
 
-        z_rows = [held("z_rows%d" % b, [P, 2, 4, HALF], BF16) for b in range(2)]
-
         def larger(i, lo, hi):
             one, two = picks[i, lo]
-            halves = slice(lo // HALF, hi // HALF)
-            nc.vector.tensor_tensor(
-                z_rows[i // 4][:, halves, i % 4, :],
-                one[:].rearrange("p (h c) -> p h c", c=HALF),
-                two[:].rearrange("p (h c) -> p h c", c=HALF),
-                ALU.max,
-            )
+            nc.vector.tensor_tensor(z_rows[:, i, lo:hi], one[:], two[:], ALU.max)
 
         z_round = {}
         z_mx = {}
 
-        def weave_z(b, halves, engine):
-            woven = held("z_round%d%d" % (b, halves[0]), [P, 4 * HALF * len(halves)], BF16)
+        def weave_z(b, lo, hi, engine):
+            woven = held("z_round%d%d" % (b, lo), [P, 4 * (hi - lo)], BF16)
             copy_on(
                 engine,
-                woven[:].rearrange("p (h c i t) -> p h c t i", c=HALF // 4, i=4, t=4),
-                z_rows[b][:, halves[0] : halves[-1] + 1].rearrange("p h t (c i) -> p h c t i", i=4),
+                woven[:].rearrange("p (c i t) -> p c t i", i=4, t=4),
+                z_rows[:, 4 * b : 4 * b + 4, lo:hi].rearrange("p t (c i) -> p c t i", i=4),
             )
-            z_round[b, halves[0]] = woven
+            z_round[b, lo] = woven
 
-        def quantize_z(b, halves):
-            codes, plane = quantize("z_%d%d" % (b, halves[0]), z_round[b, halves[0]][:], HALF * len(halves))
-            for n, half in enumerate(halves):
-                z_mx[b, half] = (codes[:, HALF * n : HALF * (n + 1)], plane[:, HALF * n : HALF * (n + 1)])
+        def quantize_z(b, lo, hi):
+            z_mx[b, lo] = quantize("z_%d%d" % (b, lo), z_round[b, lo][:], hi - lo)
 
         w3_round = {}
         w3_mx = {}
@@ -260,48 +243,59 @@ def tile_list_cue_crowding_scores_kernel(
 
         score = {}
 
-        def second(b, half):
-            z_codes, z_plane = z_mx[b, half]
+        def second(b, lo, hi, banks):
+            width = hi - lo
+            each = 4 // len(banks)
+            z_codes, z_plane = z_mx[b, lo * b]
+            z_cols = slice(lo, hi) if b == 0 else slice(0, width)
             codes, plane = w3_mx[b]
             for n in range(4):
-                if b == 0:
-                    score[n, half] = bank((4 + 4 * half + n) % 8, HALF)
+                if b == 0 and n % each == 0:
+                    score[lo, n // each] = bank(banks[n // each], each * width)
                 nc.tensor.matmul_mx(
-                    out=score[n, half][:],
+                    out=score[lo, n // each][:, width * (n % each) : width * (n % each + 1)],
                     lhsT=codes[:, P * n : P * (n + 1)].bitcast(FP8X4),
                     lhsT_scale=plane[:, P * n : P * (n + 1)],
-                    rhs=z_codes.bitcast(FP8X4),
-                    rhs_scale=z_plane,
-                    start=(b == 0),
-                    stop=(b == 1),
+                    rhs=z_codes[:, z_cols].bitcast(FP8X4),
+                    rhs_scale=z_plane[:, z_cols],
+                    start=(b == 0 and n % each == 0),
+                    stop=(b == 1 and n % each == each - 1),
                 )
 
-        def finish(half):
+        def finish(lo, hi, banks):
+            width = hi - lo
+            each = 4 // len(banks)
             out_rows = out.rearrange("(n p) m -> p n m", p=P)
-            for pair in range(2):
-                squared = held("squared%d%d" % (half, pair), [P, 2, HALF], F32)
-                for n in range(2):
-                    nc.scalar.activation(squared[:, n, :], score[2 * pair + n, half][:], ACT.Square)
-                nc.sync.dma_start(out_rows[:, 2 * pair : 2 * pair + 2, HALF * half : HALF * (half + 1)], squared[:])
+            for k in range(len(banks)):
+                squared = held("squared%d%d" % (lo, k), [P, each * width], F32)
+                nc.scalar.activation(squared[:], score[lo, k][:], ACT.Square)
+                nc.sync.dma_start(
+                    out_rows[:, each * k : each * (k + 1), lo:hi], squared[:].rearrange("p (n m) -> p n m", n=each)
+                )
 
         every = (0, 1, 2, 3)
-        round_w1(0, 0, every, "vector")
+        round_w1(0, 0, every, "scalar")
         curved(0)
         gain_bank = bank(0, P)
         nc.tensor.transpose(gain_bank[:], gain_rows[:], ident[:])
         nc.scalar.copy(gain_sb[:], gain_bank[:, 0:8])
         quantize_w1(0, 0, every)
+        load_w1(1, 1, "w1_round000")
         round_w1(0, 1, (0,), "vector")
         round_w1(0, 1, (1,), "scalar")
         quantize_w1(0, 1, (0,))
+        load_w1(1, 0, "w1_round010")
         linear(0)
         curved(1)
         quantize_w1(0, 1, (1,))
         linear(1)
         round_w1(0, 1, (2, 3), "scalar")
+        load_base(1, "w1_raw01")
+        load_w3(0, "w1_round011")
         features(0)
         curved(2)
         quantize_w1(0, 1, (2, 3))
+        load_w3(1, "w1_round012")
         for i in range(7):
             pick(i, 0, PAIRS)
             features(i + 1)
@@ -313,25 +307,30 @@ def tile_list_cue_crowding_scores_kernel(
             if i < 2:
                 round_w1(1, i, every, "scalar")
                 quantize_w1(1, i, every)
-            if i == 3:
-                weave_z(0, (0, 1), "scalar")
-            if i in (3, 4):
-                round_w3(i - 3)
             if i == 4:
-                quantize_z(0, (0, 1))
+                weave_z(0, 0, PAIRS, "scalar")
+                quantize_z(0, 0, PAIRS)
             if i in (4, 5):
+                round_w3(i - 4)
                 quantize_w3(i - 4)
-        second(0, 0)
-        second(0, 1)
-        pick(7, 0, HALF)
-        larger(7, 0, HALF)
-        weave_z(1, (0,), "scalar")
-        pick(7, HALF, PAIRS)
-        larger(7, HALF, PAIRS)
-        quantize_z(1, (0,))
-        weave_z(1, (1,), "vector")
-        second(1, 0)
-        finish(0)
-        quantize_z(1, (1,))
-        second(1, 1)
-        finish(1)
+        first, middle, last = (0, 256, (4, 5)), (256, 384, (6,)), (384, 512, (7, 0))
+        for piece in (first, middle, last):
+            second(0, *piece)
+        pick(7, *first[:2])
+        pick(7, *middle[:2])
+        larger(7, *first[:2])
+        weave_z(1, *first[:2], "scalar")
+        larger(7, *middle[:2])
+        weave_z(1, *middle[:2], "scalar")
+        pick(7, *last[:2])
+        quantize_z(1, *first[:2])
+        second(1, *first)
+        finish(*first)
+        larger(7, *last[:2])
+        weave_z(1, *last[:2], "vector")
+        quantize_z(1, *middle[:2])
+        second(1, *middle)
+        finish(*middle)
+        quantize_z(1, *last[:2])
+        second(1, *last)
+        finish(*last)

from contextlib import ExitStack

import concourse.mybir as mybir
from concourse.masks import make_identity

K, H, N, T, S, PAIRS = 1024, 1024, 512, 2048, 1024, 512
FLOPS = 2 * K * H * S * 2 + 2 * H * N * PAIRS

F32 = mybir.dt.float32
BF16 = mybir.dt.bfloat16
I32 = mybir.dt.int32
U32 = mybir.dt.uint32
U16 = mybir.dt.uint16
U8 = mybir.dt.uint8
FP8X4 = mybir.dt.float8_e4m3fn_x4
FP4X4 = mybir.dt.float4_e2m1fn_x4
ALU = mybir.AluOpType
ACT = mybir.ActivationFunctionType

P = 128
BANK = 512
HALF = PAIRS // 2


def tile_list_cue_crowding_scores_kernel(
    tc, tab_words, tab_scales, offs, pos1, pos2, w1, w2_words, w2_scales, gain, base, w3, out
):
    nc = tc.nc
    with ExitStack() as ctx:
        keep = ctx.enter_context(tc.tile_pool(name="keep", bufs=1))
        ring = ctx.enter_context(tc.tile_pool(name="ring", bufs=2))
        psum = ctx.enter_context(tc.psum_pool(name="psum", bufs=1))

        def held(name, shape, dtype, slot=None):
            return keep.tile(shape, dtype, name=name, tag=slot or name, align_bytes=64)

        def bank(n, width=BANK):
            return psum.tile([P, width], F32, name="bank%d" % n, tag="bank%d" % n)

        def slot_rows(x, b, t):
            return x[512 * b : 512 * (b + 1), :].rearrange("(g t q) m -> g t q m", t=4, q=8)[:, t, :, :]

        offs_sb = held("offs_sb", [P, S // 16], U16)
        pos1_sb = held("pos1_sb", [P, PAIRS // 16], U16)
        pos2_sb = held("pos2_sb", [P, PAIRS // 16], U16)
        nc.sync.dma_start(offs_sb[:], offs)
        nc.sync.dma_start(pos1_sb[:], pos1)
        nc.sync.dma_start(pos2_sb[:], pos2)

        tab_rows = held("tab_rows", [P, T], U8)
        w2_rows = held("w2_rows", [P, 2 * H], U8)
        gain_rows = held("gain_rows", [P, P], F32)
        v_planes = held("v_planes", [P, 2 * S], U8)
        nc.gpsimd.memset(tab_rows[:].bitcast(I32), 0)
        nc.gpsimd.memset(w2_rows[:].bitcast(I32), 0)
        nc.gpsimd.memset(gain_rows[:], 0.0)
        nc.gpsimd.memset(v_planes[:].bitcast(I32), 0)
        ident = held("ident", [P, P], F32)
        make_identity(nc, ident[:])
        nc.scalar.dma_start(tab_rows[0:P:4, :].bitcast(I32), tab_scales.rearrange("a q t -> q a t").bitcast(I32))
        for d in range(4):
            nc.scalar.dma_start(
                w2_rows[32 * d : 32 * d + 4, :].bitcast(I32).rearrange("r (a c) -> r a c", a=2),
                w2_scales[:, 4 * d : 4 * d + 4, :].rearrange("a r c -> r a c").bitcast(I32),
            )
        for b in range(2):
            nc.scalar.dma_start(
                gain_rows[4 * b : 4 * b + 4, :].rearrange("t (g q) -> t g q", q=8),
                gain[512 * b : 512 * (b + 1)].rearrange("(g t q) -> t g q", t=4, q=8),
            )

        tab_sb = {}

        def load_table(a):
            tab_sb[a] = held("tab_sb%d" % a, [P, T], I32)
            nc.sync.dma_start(tab_sb[a][:], tab_words[a].rearrange("p t i -> p (t i)").bitcast(I32))

        w1_raw = {}
        base_sb = {}
        w3_raw = {}

        def load_w1(b, a, slot=None):
            w1_raw[b, a] = held("w1_raw%d%d" % (b, a), [P, 4, 512], F32, slot)
            rows = w1[512 * a : 512 * (a + 1), 512 * b : 512 * (b + 1)]
            nc.sync.dma_start(w1_raw[b, a][:], rows.rearrange("(p j) c -> p j c", j=4))

        def load_base(b, slot):
            rows = held("base_sb%d" % b, [P, 4, PAIRS], F32, slot)
            for t in range(4):
                base_sb[4 * b + t] = rows[:, t, :]
                nc.sync.dma_start(rows[:, t, :], slot_rows(base, b, t))

        def load_w3(b, slot):
            w3_raw[b] = held("w3_raw%d" % b, [P, 4, N], F32, slot)
            for t in range(4):
                nc.sync.dma_start(w3_raw[b][:, t, :], slot_rows(w3, b, t))

        load_table(0)
        load_w1(0, 0)
        load_table(1)
        w2_raw = held("w2_raw", [P, H], I32)
        nc.sync.dma_start(w2_raw[:].rearrange("p (a c) -> p a c", a=2), w2_words.rearrange("a p c -> p a c").bitcast(I32))
        load_w1(0, 1)

        picked_rows = held("picked_rows", [P, S], U8)
        nc.vector.tensor_copy(picked_rows[:], tab_rows[:].indirect(offs_sb[:]))
        for d in range(4):
            nc.scalar.dma_start(
                v_planes[32 * d : 32 * d + 4, :].bitcast(I32).rearrange("r (a s) -> r a s", a=2),
                picked_rows[32 * d : 32 * (d + 1) : 4, :].bitcast(I32),
            )
        v_words = []
        for a in range(2):
            picked = held("v_words%d" % a, [P, S], U32)
            nc.vector.tensor_copy(picked[:], tab_sb[a][:].bitcast(U32).indirect(offs_sb[:]))
            v_words.append(picked)

        w2_codes = held("w2_codes", [P, 4 * H], U8)
        nc.vector.tensor_copy(
            w2_codes[:].bitcast(I32).rearrange("p (c t g w) -> p c t g w", t=4, g=16, w=4),
            w2_raw[:].rearrange("p (c g t w) -> p c t g w", t=4, g=16, w=4),
        )
        w2_planes = held("w2_planes", [P, 2 * H], U8)
        nc.vector.tensor_copy(
            w2_planes[:].bitcast(I32).rearrange("p (c t g w) -> p c t g w", t=4, g=16, w=2),
            w2_rows[:].bitcast(I32).rearrange("p (c g t w) -> p c t g w", t=4, g=16, w=2),
        )

        load_base(0, "picked_rows")
        gain_sb = held("gain_sb", [P, 8], F32)

        def copy_on(engine, dst, src):
            if engine == "vector":
                nc.vector.tensor_copy(dst, src)
            else:
                nc.scalar.copy(dst, src)

        def quantize(name, rounded, width):
            codes = held(name + "_codes", [P, width], U32)
            plane = held(name + "_plane", [P, width], U8)
            nc.vector.quantize_mx(out=codes[:].bitcast(FP8X4), scales=plane[:], in_=rounded)
            return codes, plane

        w1_round = {}
        w1_mx = {}

        def round_w1(b, a, slots, engine):
            rounded = held("w1_round%d%d%d" % (b, a, slots[0]), [P, 512 * len(slots)], BF16)
            src = w1_raw[b, a][:].rearrange("p j (g t u i) -> p t g u j i", t=4, u=2, i=4)
            for n, t in enumerate(slots):
                dst = rounded[:, 512 * n : 512 * (n + 1)].rearrange("p (g u i j) -> p g u j i", u=2, i=4, j=4)
                copy_on(engine, dst, src[:, t])
            w1_round[b, a, slots[0]] = rounded

        def quantize_w1(b, a, slots):
            codes, plane = quantize("w1_%d%d%d" % (b, a, slots[0]), w1_round[b, a, slots[0]][:], P * len(slots))
            for n, t in enumerate(slots):
                w1_mx[4 * b + t, a] = (codes[:, P * n : P * (n + 1)], plane[:, P * n : P * (n + 1)])

        def product(acc, lhs, lhs_plane, a, c):
            nc.tensor.matmul_mx(
                out=acc[:],
                lhsT=lhs,
                lhsT_scale=lhs_plane,
                rhs=v_words[a][:, BANK * c : BANK * (c + 1)].bitcast(FP8X4),
                rhs_scale=v_planes[:, S * a + BANK * c : S * a + BANK * (c + 1)],
                start=(a == 0),
                stop=(a == 1),
            )

        curve = held("curve", [P, 9 * S], F32)
        silu_sb = [curve[:, S * i : S * (i + 1)] for i in range(8)]
        z_rows = curve[:, S:].bitcast(BF16).rearrange("p (i m) -> p i m", i=8)
        lin = {}
        h_sb = {}
        picks = {}

        def curved(i):
            for c in range(2):
                acc = bank(4 + 2 * (i % 2) + c)
                for a in range(2):
                    col = H * a + P * i
                    product(acc, w2_codes[:, 2 * col : 2 * (col + P)].bitcast(FP4X4), w2_planes[:, col : col + P], a, c)
                nc.scalar.activation(silu_sb[i][:, BANK * c : BANK * (c + 1)], acc[:], ACT.Silu)

        def linear(i):
            for c in range(2):
                lin[i, c] = bank(2 * (i % 2) + c)
                for a in range(2):
                    codes, plane = w1_mx[i, a]
                    product(lin[i, c], codes.bitcast(FP8X4), plane, a, c)

        def features(i):
            h_sb[i] = ring.tile([P, S], F32, name="h_sb", bufs=3, align_bytes=64)
            for c in range(2):
                cols = slice(BANK * c, BANK * (c + 1))
                nc.vector.scalar_tensor_tensor(
                    h_sb[i][:, cols], silu_sb[i][:, cols], gain_sb[:, i : i + 1], lin[i, c][:], ALU.mult, ALU.add
                )

        def pick(i, lo, hi):
            both = []
            for name, pos in (("pick1", pos1_sb), ("pick2", pos2_sb)):
                got = ring.tile([P, hi - lo], F32, name=name, bufs=3, align_bytes=64)
                nc.vector.tensor_tensor(
                    got[:], h_sb[i][:].indirect(pos[:, lo // 16 : hi // 16]), base_sb[i][:, lo:hi], ALU.subtract
                )
                both.append(got)
            picks[i, lo] = both

        def larger(i, lo, hi):
            one, two = picks[i, lo]
            nc.vector.tensor_tensor(z_rows[:, i, lo:hi], one[:], two[:], ALU.max)

        z_round = {}
        z_mx = {}

        def weave_z(b, lo, hi, engine):
            woven = held("z_round%d%d" % (b, lo), [P, 4 * (hi - lo)], BF16)
            copy_on(
                engine,
                woven[:].rearrange("p (c i t) -> p c t i", i=4, t=4),
                z_rows[:, 4 * b : 4 * b + 4, lo:hi].rearrange("p t (c i) -> p c t i", i=4),
            )
            z_round[b, lo] = woven

        def quantize_z(b, lo, hi):
            z_mx[b, lo] = quantize("z_%d%d" % (b, lo), z_round[b, lo][:], hi - lo)

        w3_round = {}
        w3_mx = {}

        def round_w3(b):
            w3_round[b] = held("w3_round%d" % b, [P, 4 * N], BF16)
            for c in range(2):
                nc.scalar.copy(
                    w3_round[b][:, 2 * N * c : 2 * N * (c + 1)].rearrange("p (c i t) -> p c t i", i=4, t=4),
                    w3_raw[b][:, :, N // 2 * c : N // 2 * (c + 1)].rearrange("p t (c i) -> p c t i", i=4),
                )

        def quantize_w3(b):
            w3_mx[b] = quantize("w3_%d" % b, w3_round[b][:], N)

        score = {}

        def second(b, lo, hi, banks):
            width = hi - lo
            each = 4 // len(banks)
            z_codes, z_plane = z_mx[b, lo * b]
            z_cols = slice(lo, hi) if b == 0 else slice(0, width)
            codes, plane = w3_mx[b]
            for n in range(4):
                if b == 0 and n % each == 0:
                    score[lo, n // each] = bank(banks[n // each], each * width)
                nc.tensor.matmul_mx(
                    out=score[lo, n // each][:, width * (n % each) : width * (n % each + 1)],
                    lhsT=codes[:, P * n : P * (n + 1)].bitcast(FP8X4),
                    lhsT_scale=plane[:, P * n : P * (n + 1)],
                    rhs=z_codes[:, z_cols].bitcast(FP8X4),
                    rhs_scale=z_plane[:, z_cols],
                    start=(b == 0 and n % each == 0),
                    stop=(b == 1 and n % each == each - 1),
                )

        def finish(lo, hi, banks):
            width = hi - lo
            each = 4 // len(banks)
            out_rows = out.rearrange("(n p) m -> p n m", p=P)
            for k in range(len(banks)):
                squared = held("squared%d%d" % (lo, k), [P, each * width], F32)
                nc.scalar.activation(squared[:], score[lo, k][:], ACT.Square)
                nc.sync.dma_start(
                    out_rows[:, each * k : each * (k + 1), lo:hi], squared[:].rearrange("p (n m) -> p n m", n=each)
                )

        every = (0, 1, 2, 3)
        round_w1(0, 0, every, "scalar")
        curved(0)
        gain_bank = bank(0, P)
        nc.tensor.transpose(gain_bank[:], gain_rows[:], ident[:])
        nc.scalar.copy(gain_sb[:], gain_bank[:, 0:8])
        quantize_w1(0, 0, every)
        load_w1(1, 1, "w1_round000")
        round_w1(0, 1, (0,), "vector")
        round_w1(0, 1, (1,), "scalar")
        quantize_w1(0, 1, (0,))
        load_w1(1, 0, "w1_round010")
        linear(0)
        curved(1)
        quantize_w1(0, 1, (1,))
        linear(1)
        round_w1(0, 1, (2, 3), "scalar")
        load_base(1, "w1_raw01")
        load_w3(0, "w1_round011")
        features(0)
        curved(2)
        quantize_w1(0, 1, (2, 3))
        load_w3(1, "w1_round012")
        for i in range(7):
            pick(i, 0, PAIRS)
            features(i + 1)
            if i + 2 < 8:
                linear(i + 2)
            if i + 3 < 8:
                curved(i + 3)
            larger(i, 0, PAIRS)
            if i < 2:
                round_w1(1, i, every, "scalar")
                quantize_w1(1, i, every)
            if i == 4:
                weave_z(0, 0, PAIRS, "scalar")
                quantize_z(0, 0, PAIRS)
            if i in (4, 5):
                round_w3(i - 4)
                quantize_w3(i - 4)
        first, middle, last = (0, 256, (4, 5)), (256, 384, (6,)), (384, 512, (7, 0))
        for piece in (first, middle, last):
            second(0, *piece)
        pick(7, *first[:2])
        pick(7, *middle[:2])
        larger(7, *first[:2])
        weave_z(1, *first[:2], "scalar")
        larger(7, *middle[:2])
        weave_z(1, *middle[:2], "scalar")
        pick(7, *last[:2])
        quantize_z(1, *first[:2])
        second(1, *first)
        finish(*first)
        larger(7, *last[:2])
        weave_z(1, *last[:2], "vector")
        quantize_z(1, *middle[:2])
        second(1, *middle)
        finish(*middle)
        quantize_z(1, *last[:2])
        second(1, *last)
        finish(*last)
